import numpy as np, ml_dtypes
CORES = [23,119,17,113]
N = 4
BF = ml_dtypes.bfloat16
def gentries(a):
    return np.ascontiguousarray(a.reshape(8, 16, -1).transpose(0, 2, 1)).reshape(8, -1)
def gtable(e):
    e = np.asarray(e); return np.ascontiguousarray(e.reshape(8, -1, 16).transpose(0, 2, 1)).reshape(128, -1).astype(np.int32)
V, L, CAP, RO, LO, HI = 4096, 128, 256, 3, 200, 480
SHIFTS = (1,)
GH = L * len(SHIFTS)
SZ = np.array([LO // 20, (LO + HI) // 16, HI // 5, 127])
def fold(v):
    return np.abs((v + 127) % 508 - 254) - 127
def steps(rng, a, b):
    u = rng.random((N, 8, 1, V)); w = np.where(u < a, SZ[0], np.where(u < 1 - b, SZ[1], np.where(u < 1 - 0.4 * b, SZ[2], SZ[3])))
    return fold(rng.integers(-127, 128, (N, 8, 16, 1)) + np.add.accumulate(rng.integers(-w, w + 1, (N, 8, 16, V)), axis=3))
def walk(rng, t):
    i = np.arange(16); m = t[..., None] // 16 + ((i + np.arange(V)[:, None]) % 16 < t[..., None] % 16)
    kind = rng.integers(0, 4, t.shape); s = (kind == 1) & (t > 259); one = kind == 2
    four = np.stack([i // 4 == h for h in range(4)] + [i % 4 == h for h in range(4)]); u = rng.integers(0, 8, np.count_nonzero(s))
    fin = np.add.accumulate(four.astype(np.int64), axis=1) - 1; fout = np.add.accumulate((~four).astype(np.int64), axis=1) - 1
    a = 257 + 2 * rng.integers(0, 2, (u.size, 1)); b = t[s][:, None] - a
    m[s] = np.where(four[u], a // 4 + (fin[u] < a % 4), b // 12 + (fout[u] < b % 12))
    y = np.zeros((N, 8, 16, V), np.int64); p = rng.integers(-127, 128, (N, 8, 16)); z = 2 * rng.integers(0, 2, (V, N, 8, 16)) - 1
    for k in range(V):
        y[..., k] = p; tk = t[:, :, k, None]; h = np.abs(p)
        big = np.minimum(tk, 127 + np.max(h, axis=2, keepdims=True)); w = tk - big; o = (i - np.argmax(h, axis=2)[..., None]) % 16
        mk = np.where(one[:, :, k, None], np.where(o == 0, big, w // 15 + (o <= w % 15)), m[:, :, k])
        p = p + mk * np.where(np.abs(p + z[k] * mk) <= 127, z[k], np.where(p > 0, -1, 1))
    return y
def lay(rng, y, n, m, mode, ok):
    x = np.zeros((N, 8, 16, V), np.int64); nx = np.full((N, 8, V), -1, np.int64); hd = np.zeros((N, 8, GH), np.int64)
    for q in range(N):
        for g in range(8):
            k, mm, o = int(n[q, g]), int(m[q, g]), rng.permutation(V)
            if mode[q, g] == 1: o = np.concatenate([V - k + rng.permutation(k), rng.permutation(V - k)])
            if mode[q, g] == 2: o = np.concatenate([rng.permutation(k), k + rng.permutation(V - k)])
            if mode[q, g] == 3:
                o = np.concatenate([rng.permutation(V - 1), np.full(1, V - 1)])
                o = np.concatenate([o[:k][o[:k] % 2 == 1], o[:k][o[:k] % 2 == 0], o[k:]])
            if mode[q, g] == 4:
                ev, od, w = 2 * rng.permutation(V // 2), 2 * rng.permutation(V // 2) + 1, k // 2
                o = np.concatenate([np.stack([ev[:w], od[:w]], axis=1).reshape(-1), rng.permutation(np.concatenate([ev[w:], od[w:]]))])
            if mode[q, g] == 5:
                z = rng.permutation(16)[np.arange(V) % 16]; fr = z == 15
                fr[np.flatnonzero((z > 1) & (z < 15))[-(V - k - V // 16):]] = True
                lv = rng.permutation(np.flatnonzero(~fr)); lv = lv[np.argsort(z[lv], kind="stable")]
                a = ~ok[q, g, :k]; a = a | np.concatenate([a[1:], np.zeros(1, bool)]); c = np.count_nonzero(a)
                o[:k][a] = rng.permutation(lv[:c]); o[:k][~a] = rng.permutation(lv[c:]); o[k:] = np.flatnonzero(fr)
            x[q, g][:, o] = y[q, g]
            u = o[:k]; c = np.sort(rng.permutation(k - 1)[:mm - 1]) + 1
            a = np.concatenate([np.zeros(1, np.int64), c]); b = np.concatenate([c, np.full(1, k)]) - 1
            e = min((mm + 1) // 2 + int(rng.integers(0, mm // 2 + 1)), GH)
            nx[q, g, u[:-1]] = u[1:]; nx[q, g, u[b]] = u[a]
            nx[q, g, u[b[rng.permutation(mm)[:e]]]] = V + rng.permutation(GH)[:e]
            h = u[(u % 2 == 0) & ok[q, g, :k]]; d = rng.permutation(h[nx[q, g, h] >= V])[:GH // 4]
            hd[q, g] = rng.permutation(np.resize(np.concatenate([d, rng.permutation(np.setdiff1d(h, d))]), GH))
    return x, nx, hd
def nears(rng, x, nx, hd):
    for q in range(N):
        for g in range(8):
            i = rng.permutation(np.flatnonzero(nx[q, g] >= V)); i = i[:(i.size + 1) // 2]
            if i.size == 0: continue
            t = nx[q, g, i] - V; src = (q + np.array(SHIFTS)[t // L]) % N
            w = SZ[rng.integers(0, 3, (i.size, 1))]
            x[q, g][:, i] = np.clip(x[src, g, :, hd[src, g, t]] + rng.integers(-w, w + 1, (i.size, 16)), -127, 127).T
def off(rng, p, t):
    m = t[:, None] // 16 + ((np.arange(16) + rng.integers(0, 16, (t.size, 1))) % 16 < t[:, None] % 16)
    z = 2 * rng.integers(0, 2, p.shape) - 1
    return p + m * np.where(np.abs(p + z * m) <= 127, z, np.where(p > 0, -1, 1))
def edge(rng, x, nx, hd):
    for q in range(N):
        for g in range(8):
            i = np.flatnonzero((nx[q, g] >= V) & ~np.isin(np.arange(V), hd[q, g]))
            if i.size == 0: continue
            t = nx[q, g, i] - V; src = (q + np.array(SHIFTS)[t // L]) % N
            x[q, g][:, i] = off(rng, x[src, g, :, hd[src, g, t]], rng.choice(np.array([LO - 1, LO, HI - 1, HI, HI, HI, HI + 1, HI + 1]), i.size)).T
            before = np.full(V, -1, np.int64); own = np.flatnonzero((nx[q, g] >= 0) & (nx[q, g] < V)); before[nx[q, g, own]] = own
            b = before[i]; s = (b >= 0) & ~np.isin(b, hd[q, g])
            x[q, g][:, b[s]] = off(rng, x[q, g][:, i[s]].T, rng.choice(np.array([0, 1, LO // 2, LO - 1, LO - 1, LO]), np.count_nonzero(s))).T
def pack(x, nx, hd):
    return {"x": np.ascontiguousarray(x.reshape(N, 128, V)).astype(np.float32).astype(BF), "nxt": np.stack([gtable(a) for a in nx]), "head": np.stack([gtable(a) for a in hd])}
def sizes(rng):
    return rng.integers(V // 2, V - RO * CAP + 1, (N, 8)), rng.integers(GH // 2, GH + 33, (N, 8))
ANY = np.ones((N, 8, V), bool); MIX = np.zeros((N, 8), np.int64)
def setup_inputs(rng):
    n, m = sizes(rng); a = rng.choice(np.array([0.25, 0.35, 0.5]), (N, 8, 1, 1)); b = rng.choice(np.array([0.02, 0.06, 0.12, 0.25]), (N, 8, 1, 1))
    x, nx, hd = lay(rng, steps(rng, a, b), n, m, MIX, ANY); nears(rng, x, nx, hd)
    return pack(x, nx, hd)
def setup_inputs_cap(rng):
    k = V - RO * CAP; kinds = (CAP, CAP + 1, CAP - 1, 0, 1, k - 4, CAP, 0); modes = (3, 0, 0, 4, 0, 3, 5, 0)
    far = np.zeros((N, 8, V), bool); mode = np.zeros((N, 8), np.int64); m = np.ones((N, 8), np.int64); R = np.full((N, 8, 1, 1), HI // 32)
    for q in range(N):
        for g in range(8):
            j = (g + q) % 8; far[q, g, 3 + 2 * rng.permutation((k - 4) // 2)[:kinds[j] // 2]] = True
            far[q, g, 0] = kinds[j] % 2 == 1; mode[q, g] = modes[j]
            if j == 3: R[q, g] = (LO - 1) // 32
            if j == 7: far[q, g, :k - 48] = True; m[q, g] = 2 * GH
    c = rng.integers(80, 101, (8, 16, 1)) * (2 * rng.integers(0, 2, (8, 16, 1)) - 1)
    y = np.where(far[:, :, None, :], -c, c) + rng.integers(-R, R + 1, (N, 8, 16, V))
    return pack(*lay(rng, y, np.full((N, 8), k), m, mode, ~far))
def setup_inputs_ties(rng):
    n, m = sizes(rng); t = rng.choice(np.array([0, 1, LO - 1, LO, LO + 1, HI - 1, HI, HI, HI + 1, HI + 1]), (N, 8, V))
    x, nx, hd = lay(rng, walk(rng, t), n, m, MIX, ANY); edge(rng, x, nx, hd)
    return pack(x, nx, hd)
def setup_inputs_loops(rng):
    n, m = sizes(rng); m = n // 3
    x, nx, hd = lay(rng, steps(rng, 0.6, 0.1), n, m, rng.integers(0, 3, (N, 8)), ANY)
    hd[:, ::2] = np.take_along_axis(hd[:, ::2], rng.integers(0, 3, (N, 4, GH)), 2)
    q, g, z = int(rng.integers(0, N)), int(rng.integers(0, 8)), V - 2
    nx[q, g] = -1; nx[q, g, z] = z; hd[q, g] = z
    nears(rng, x, nx, hd)
    return pack(x, nx, hd)
def setup_inputs_churn(rng):
    n, m = sizes(rng); n[:, ::2] = V - RO * CAP
    x, nx, hd = lay(rng, steps(rng, 0.55, 0.35), n, m, rng.integers(0, 3, (N, 8)), ANY); nears(rng, x, nx, hd)
    return pack(x, nx, hd)
def setup_inputs_spread(rng):
    n, m = sizes(rng); y = np.rint(127 * np.exp2(-7 * rng.random((N, 8, 1, V))) * (2 * rng.random((N, 8, 16, V)) - 1)).astype(np.int64)
    x, nx, hd = lay(rng, y, n, m, MIX, ANY)
    return pack(x, nx, hd)
def check_inputs(d):
    bad = []; xf = np.asarray(d["x"]).astype(np.float32)
    if not np.all(np.abs(xf) <= 127) or not np.all(np.rint(xf) == xf): bad.append("x: whole numbers from -127 to 127")
    nl = np.stack([gentries(a) for a in d["nxt"]]).astype(np.int64); hl = np.stack([gentries(a) for a in d["head"]]).astype(np.int64)
    if np.min(nl) < -1 or np.max(nl) > V + GH - 1: bad.append("range of nxt")
    if np.min(hl) < 0 or np.max(hl) > V - 1: bad.append("range of head")
    if "range of nxt" in bad or "range of head" in bad: return bad
    live = nl >= 0; own = live & (nl < V); s = np.sort(nl, axis=2)
    if np.any((s[:, :, 1:] == s[:, :, :-1]) & (s[:, :, 1:] >= 0)): bad.append("nxt: one predecessor a node")
    if np.any(own & ~np.take_along_axis(live, np.where(own, nl, 0), 2)): bad.append("nxt names live nodes only")
    if np.any(hl % 2 == 1): bad.append("heads are even")
    if not np.all(np.take_along_axis(live, hl, 2)): bad.append("heads are live")
    if np.min(np.count_nonzero(~live, axis=2)) < RO * CAP: bad.append("free nodes")
    return bad
def reference(x, nxt, head):
    X = x.astype(np.float32).astype(np.int64).reshape(N, 8, 16, V)
    nx = np.stack([gentries(a) for a in nxt]).astype(np.int64); hd = np.stack([gentries(a) for a in head]).astype(np.int64)
    even = np.arange(V) % 2 == 0
    for rnd in range(RO):
        ghost = np.stack([np.concatenate([np.take_along_axis(X[(r + s) % N], hd[(r + s) % N][:, None, b * L:(b + 1) * L], 2) for b, s in enumerate(SHIFTS)], axis=2) for r in range(N)])
        live = nx >= 0
        Xn = np.take_along_axis(np.concatenate([X, ghost], axis=3), np.where(live, nx, 0)[:, :, None, :], 3)
        ln = np.add.reduce(np.abs(X - Xn), axis=2)
        far = live & (ln > HI); split = far & (np.add.accumulate(far.astype(np.int64), axis=2) <= CAP)
        own = live & (nx < V); j = np.where(own, nx, 0)
        merge = own & even & (j % 2 == 1) & (ln < LO) & (np.take_along_axis(ln, j, 2) <= HI)
        new = np.where(merge, np.take_along_axis(nx, j, 2), nx)
        for r in range(N):
            for g in range(8):
                i = np.flatnonzero(split[r, g]); f = np.flatnonzero(~live[r, g])[:i.size]
                X[r, g][:, f] = (X[r, g][:, i] + Xn[r, g][:, i]) >> 1
                new[r, g, f] = nx[r, g, i]; new[r, g, i] = f
                new[r, g, j[r, g][merge[r, g]]] = -1
        nx = new; live = nx >= 0
        Xn = np.take_along_axis(np.concatenate([X, ghost], axis=3), np.where(live, nx, 0)[:, :, None, :], 3)
        X = X + np.where(live[:, :, None, :], np.clip(Xn - X, -1, 1), 0)
    X = np.where((nx >= 0)[:, :, None, :], X, 0)
    return {"yx": X.reshape(N, 128, V).astype(np.float32).astype(BF), "yn": np.stack([gtable(a) for a in nx]).astype(np.float32)}

from concourse.mybir import AluOpType as OP, ActivationFunctionType as AF

V, GH, RO = 4096, 128, 3
O = 256
ZC = V + GH
XW = O + ZC + 16
MAG = 25165824.0
M32 = 402653184.0
BIG = 16384.0
EARLY = 1024
COST = dict(g=1.62, s=3.95, cy=1.04, fix=40.0, pe=0.52, sem=60.0, dma=1900.0, bw=250.0, far=2600.0)
ODD, EVEN, SIGN = (512, 512, 1024), (1024, 512, 512), 0
ORDER = "6 7 0 2 1 3 5 14 15 4 17 74 18 21 19 20 22 42 96 23 97 110 16 71 98 88 40 54 99 61 11 8 9 67 10 13 100 111 112 46 113 89 114 49 115 73 84 95 180 64 102 77 189 27 33 36 26 28 32 29 25 30 39 31 34 35 38 56 37 24 57 65 55 185 191 187 70 75 58 181 59 183 190 164 132 116 148 117 133 134 149 165 118 119 150 135 136 166 151 152 137 138 120 139 153 140 167 141 121 168 142 122 154 123 143 144 124 169 170 12 103 107 108 109 106 101 104 125 155 171 172 173 156 157 174 175 126 176 177 178 179 127 145 158 159 128 129 130 131 160 146 161 162 163 147 72 60 188 182 186 184 105 62 193 203 200 206 76 194 68 204 201 192 69 207 202 205 197 208 218 211 221 224 47 87 219 209 222 225 247 220 223 226 199 196 195 210 198 48 85 212 80 52 214 213 215 230 251 216 43 227 217 229 257 255 256 63 41 90 86 53 45 81 50 262 261 263 83 51 93 94 228 259 231 232 264 258 234 267 82 66 79 260 78 248 269 268 266 236 270 44 237 91 238 265 239 271 273 275 274 272 276 285 278 286 253 249 284 277 233 250 252 254 300 280 291 289 287 282 292 295 302 290 293 235 296 303 279 240 288 299 294 304 305 297 298 281 306 283 241 307 308 301 242 311 309 243 313 314 312 310 315 316 244 317 318 334 321 322 323 340 319 335 245 337 325 324 341 338 336 327 354 328 246 339 355 357 360 342 331 356 343 358 361 330 333 329 344 347 348 332 359 362 350 349 351 320 443 326 345 353 352 363 365 383 391 392 393 346 399 397 398 400 394 366 395 364 367 396 368 401 402 92 403 405 404 444 406 370 407 408 410 414 372 409 373 411 374 415 375 412 387 385 369 420 413 388 384 386 436 421 416 422 418 427 417 389 390 435 428 423 425 424 429 371 431 419 432 438 426 430 437 433 446 445 440 434 376 439 377 442 441 378 447 448 379 455 449 451 454 453 452 450 380 456 457 458 474 460 381 459 461 462 463 480 464 475 465 467 476 477 481 494 478 479 466 468 495 486 497 500 482 483 498 489 501 469 382 470 484 473 527 496 471 499 487 488 485 472 502 525 523 583 490 528 491 503 492 493 505 531 532 533 539 584 537 538 541 504 506 535 507 534 540 509 526 536 524 542 543 545 544 511 546 516 517 547 548 550 551 554 549 552 518 508 510 553 519 512 513 555 514 557 515 559 529 560 577 520 576 521 530 586 585 556 567 561 568 562 571 558 572 569 563 565 522 588 564 573 578 579 592 589 570 566 574 580 575 581 590 582 593 594 587 602 603 604 656 657 605 606 658 607 608 638 609 610 611 612 613 614 615 659 620 616 617 660 639 640 621 641 622 661 662 623 624 642 643 663 618 591 625 664 665 644 645 626 646 647 627 648 628 619 649 629 650 651 652 653 630 666 667 668 669 631 632 670 633 634 635 671 654 595 636 655 596 672 597 598 599 600 637 673 601"

SCRATCH = {}
def _s(names, shape, d, where="sbuf"):
    for n in names.split():
        SCRATCH[n] = (where, [128, shape], d)
_s("X0 X1 X2 X3", XW, "bfloat16")
_s("D", O + V, "bfloat16")
_s("A C S0 S1 S2", V, "bfloat16")
_s("D2 WG BSEL", 2048, "bfloat16")
_s("W", ZC + 256, "bfloat16")
_s("Z0 Z1 Z2", 2048 + V, "float32")
_s("NX", 256, "int32"); _s("HD PI", 8, "int32"); _s("HO HA", 8, "uint16"); _s("HF HG", 8, "float32")
_s("NF N ZL ZERO YL YO N2", 256, "float32")
_s("PERM PINV H ZV", 512, "float32")
_s("ONEF IDF THO T1 T2 T3 M8 NM DL DUM", 128, "float32")
_s("E1 E2 VAL FL1 FL2", 512, "bfloat16")
_s("FL3", 1024, "bfloat16")
_s("NROW NH NL OK LIVE PADC HU", 256, "bfloat16")
_s("SEL S32 SW SN SP SM", 144, "bfloat16")
_s("TW", 288, "bfloat16"); _s("RY", 288, "float32"); _s("CUM", 304, "bfloat16"); _s("FG", 576, "bfloat16")
_s("LLE LGT ONE ID IDM IDK I128 I32 NOTS NOTO U1 U2 U3 GA G0 G1 G2 LA LB", 128, "bfloat16")
_s("OFF", 256, "uint16"); _s("SIG OF2 ZO", 128, "uint16")
_s("OD OC OV OS", 32, "uint16")
_s("COL E16 NLI K1 K2 LV LS Q", 16, "float32")
_s("BV BS VV SS", 32, "float32")
_s("P0 P1 P2 P3 P4 P5 P6 P7", 512, "float32", "psum")

NDMA = 48
SEMAPHORES = ["eG", "eV", "eS", "eP", "sent", "arrA", "arr0", "arr1", "arr2"] + ["d%d" % i for i in range(NDMA)]


def meet(a, b):
    if a[2] <= b[1] or b[2] <= a[1]: return False
    if a[3] is not None and b[3] is not None and a[3] != b[3]: return False
    if a[4] is not None and b[4] is not None and a[4] != b[4]: return False
    return True


def depends(ops):
    hist = {}; res = []
    for i, (q, kind, call, rd, wr, cost) in enumerate(ops):
        deps = set()
        for regs, w in ((rd, False), (wr, True)):
            for r in regs:
                psum = r[0][0] == "P" and r[0][1:].isdigit()
                for (j, r2, w2) in hist.get(r[0], []):
                    if (psum and (ops[j][0] != q or q == "P")) or ((w or w2) and meet(r, r2)): deps.add(j)
        res.append(deps)
        for r in rd: hist.setdefault(r[0], []).append((i, r, False))
        for r in wr: hist.setdefault(r[0], []).append((i, r, True))
    return res


def arrange(ops, order):
    order = [int(x) for x in order.split()] or list(range(len(ops)))
    at = {j: k for k, j in enumerate(order)}
    assert len(at) == len(ops) and all(at[j] < at[i] for i, d in enumerate(depends(ops)) for j in d)
    return [ops[i] for i in order]


def emit(g, T, ops):
    Q = {"G": g, "V": g.vector, "S": g.scalar, "P": g.tensor, "Y": g.sync}
    known = {q: {} for q in "GVSPYA"}; clock = []; waits = []; key = []
    for i, deps in enumerate(depends(ops)):
        q, kind = ops[i][:2]; kn = known[q]; need = []
        for j in sorted(deps, reverse=True):
            if kind == "arrive" or q == ops[j][0] == "P" or ops[j][4][0][0][:3] == "out" or kn.get(key[j], -1) >= j: continue
            need.append(j)
            for k, v in clock[j].items():
                if kn.get(k, -1) < v: kn[k] = v
        waits.append(need)
        key.append(q if kind == "c" else "x%d" % i)
        c = dict(kn); c[key[i]] = i; clock.append(c)
    marked = set(j for n in waits for j in n)
    sig = {}; cnt = {q: 0 for q in Q}; nd = 0; tail = []
    for i, (q, kind, call, rd, wr, cost) in enumerate(ops):
        if kind == "c":
            if i in marked:
                cnt[q] += 1; sig[i] = (T.sem["e" + q], cnt[q])
        elif kind == "dma":
            sig[i] = (T.sem["d%d" % nd], 16); nd += 1
            if i not in marked: tail.append(i)
        else:
            sig[i] = call
    for i, (q, kind, call, rd, wr, cost) in enumerate(ops):
        for j in waits[i]: Q[q].wait_ge(sig[j][0], sig[j][1])
        if kind == "c":
            ins = call(Q[q])
            if i in sig: ins.then_inc(sig[i][0], 1)
        elif kind == "dma":
            call(Q[q]).then_inc(sig[i][0], 16)
    for i in tail: g.sync.wait_ge(sig[i][0], 16)


def rank_program(g, core, T, topo):
    rank = T.rank_of(core)
    if rank is None:
        return
    cores = T.cores
    dst = cores[(rank - 1) % len(cores)]; src = cores[(rank + 1) % len(cores)]
    rid, pid = topo.addr(dst)[:2]
    mask = topo.mask(core, dst); n_out = len(topo.engines(core, dst)); n_in = len(topo.engines(src, core))
    ops = []

    def v(name, lo=0, hi=None, step=1, p=None):
        t = T[name]; hi = t.shape[1] if hi is None else hi
        cs = slice(lo, hi, step) if step > 1 else slice(lo, hi)
        ap = t[:, cs] if p is None else t[p::16, cs]
        wide = 2 if SCRATCH[name][2] in ("bfloat16", "uint16") else 4
        return (ap, [(name, lo, hi, lo % 2 if step % 2 == 0 else None, p, len(range(lo, hi, step)), wide)])
    def ind(win, off): return (win[0].indirect(off[0]), win[1], off[1])
    def add(q, kind, call, out, ins, cost=None, full=1):
        rd = []
        for a in ins + ([(0, out[2])] if len(out) == 3 else []):
            if isinstance(a, tuple): rd += a[1] + (a[2] if len(a) == 3 else [])
        if cost is None:
            n = out[1][0][5]; sides = [out] + ins[:full]
            if len(out) == 3: cost = 50 + 16 * out[2][0][5] * COST["s"]
            elif ins and len(ins[0]) == 3: cost = 50 + n * COST["g"]
            else:
                f = 0.5 if q == "V" and all(a[1][0][6] == 2 for a in sides) else 1.0
                if full == 2: f = 1.0 if any(SCRATCH[a[1][0][0]][0] == "psum" for a in ins[:2]) else 2.0
                cost = COST["fix"] + max(64, n * f) * COST["cy"]
        ops.append((q, kind, call, rd, out[1], cost))
    def ap(a): return a[0] if isinstance(a, tuple) else a
    def cp(out, a): add("V", "c", lambda e: e.tensor_copy(out[0], a[0]), out, [a])
    def ms(out, c): add("V", "c", lambda e: e.memset(out[0], c), out, [])
    def tt(out, a, b, op): add("V", "c", lambda e: e.tensor_tensor(out[0], a[0], b[0], op), out, [a, b], None, 2)
    def ts(out, a, s1, o1, s2=None, o2=None):
        if o2 is None: add("V", "c", lambda e: e.tensor_scalar(out[0], a[0], ap(s1), None, o1), out, [a, s1])
        else: add("V", "c", lambda e: e.tensor_scalar(out[0], a[0], ap(s1), ap(s2), o1, o2), out, [a, s1, s2])
    def act(out, a, f=AF.Copy, **k):
        add("S", "c", lambda e: e.activation(out[0], a[0], f, **{n: ap(x) for n, x in k.items()}), out, [a] + list(k.values()))
    def mm(out, pairs, first=True, last=True):
        def call(e):
            for i, (l, r) in enumerate(pairs): ins = e.matmul(out[0], l[0], r[0], first and i == 0, last and i == len(pairs) - 1)
            return ins
        add("P", "c", call, out, [a for p in pairs for a in p], sum(5 + max(64, r[1][0][5]) * COST["pe"] * (r[1][0][6] // 2) ** 2 for l, r in pairs))
    def dma(q, out, a, size, after=()): add(q, "dma", lambda e: e.dma_start(out[0], a[0]), out, [a] + list(after), COST["dma"] + size / COST["bw"])
    def hbm(name, lo=0, hi=None): return (T[name][:, lo:hi] if hi else T[name][:], [(name, lo, hi or 1 << 20, None, None, 0, 0)])
    def iota(out, pat, base, cm, flag=True):
        c = 130 + 2 * out[1][0][5] * COST["cy"]
        if flag: add("G", "c", lambda e: e.iota(out[0], pat, base, cm, allow_small_or_imprecise_dtypes=True), out, [], c)
        else: add("G", "c", lambda e: e.iota(out[0], pat, base, cm), out, [], c)
    def asel(out, pat, base, after=()):
        add("G", "c", lambda e: e.affine_select(out[0], T.ONEF[:], pat, OP.is_equal, 0.0, base, -1), out, [v("ONEF")] + list(after), 440.0)
    def sel(r, name="SEL"): return v(name, 15 - r, 143 - r)
    def rows(name, lo, n, w="SEL"): return [(sel(r, w), v(name, lo + r, lo + n, 16)) for r in range(16)]
    def col(i): return v("COL", i, i + 1)
    def nodes(X, b, lo, n):
        o = 0 if X[0] == "S" else O
        return v(X, o + 2 * lo + b, o + 2 * (lo + n), 2)
    def mark(name): return (0, [(name, 0, 1, None, None, 1, 4)])
    def pieces(sizes): return [(sum(sizes[:i]), n) for i, n in enumerate(sizes)]

    def send(tag, land, after=()):
        G = v("G" + tag)
        add("G", "c", lambda e: e.remote_dma(land[0], G[0], T.sem["arr" + tag], T.sem.sent, pid, rid, mask), mark("out" + tag), [G] + list(after), 500.0)
        add("A", "arrive", (T.sem["arr" + tag], n_in), land, [mark("out" + tag)], COST["far"] * (2 if tag == "A" else 1))
    def spread(b, k):
        for r in range(16):
            mm(v("P%d" % (4 + k), r, 512, 16), [(v("BSEL", 128 * r, 128 * r + 128), v("LIVE", 128 * b + 32 * k, 128 * b + 32 * k + 32))])

    dma("Y", v("HD"), hbm("head"), 4096); dma("Y", v("X0", O, O + EARLY), hbm("x", 0, EARLY), EARLY << 8)
    dma("Y", v("NX"), hbm("nxt"), 1 << 17); dma("Y", v("X0", O + EARLY, O + V), hbm("x", EARLY, V), (V - EARLY) << 8)
    ms(v("ONEF"), 1.0); ms(v("ZERO"), 0.0)
    iota(v("PI", 0, 1), [[0, 1]], 0, 1, False)
    iota(v("NROW"), [[1, 256]], 0, 0)
    for b in range(2):
        for h in range(2):
            asel(v("PERM", 128 * (2 * b + h), 128 * (2 * b + h + 1)), [[16, 8], [1000, 2], [2, 8]], b - 1000 * h)
    iota(v("NLI"), [[16, 16]], 0, 0); iota(v("DUM"), [[16, 128]], -2048, 0)
    ts(v("PI", 2, 3), v("PI", 0, 1), 112, OP.bitwise_and); ts(v("PI", 4, 5), v("PI", 0, 1), 15, OP.bitwise_and)
    cp(col(0), v("PI", 0, 1)); cp(col(1), v("PI", 2, 3)); cp(col(2), v("PI", 4, 5))
    ts(col(3), col(1), 15.0, OP.add)
    J = v("NROW", 0, 128)
    ts(v("E16"), v("NROW", 0, 16), col(2), OP.is_equal)
    ts(v("U1"), J, col(1), OP.is_ge); ts(v("U2"), J, col(3), OP.is_le); tt(v("ONE"), v("U1"), v("U2"), OP.mult)
    for r in range(16): act(v("BSEL", 128 * r, 128 * r + 128), v("ONE"), scale=v("E16", r, r + 1))
    for i, c in ((8, -(V - 1.0)), (10, -199.0), (11, -480.0), (12, -MAG), (13, -MAG / 2), (14, 32.0), (15, -M32)): ms(col(i), c)
    ms(v("HG", 0, 1), -(ZC - 1.0)); ms(v("HG", 1, 2), 480.0)
    ts(v("SEL"), v("NROW", 0, 144), col(3), OP.is_equal)
    ts(v("U3"), J, col(0), OP.is_ge, 2.0, OP.mult); tt(v("LLE"), v("U3"), v("ONE"), OP.mult)
    ts(v("U1"), J, col(0), OP.is_lt, 2.0, OP.mult); tt(v("LGT"), v("U1"), v("ONE"), OP.mult)
    ts(v("ID"), J, col(0), OP.is_equal); act(v("IDF"), v("ID"))
    for n, c in (("IDM", -1.0), ("IDK", -BIG), ("I128", 128.0), ("I32", 1.0 / 32)): act(v(n), v("ID"), scale=c)
    tt(col(4), v("E16", 0, 1), v("E16", 1, 2), OP.add); ts(col(9), v("E16", 2, 3), -BIG, OP.mult); tt(col(5), col(9), col(4), OP.add)
    ts(col(6), col(2), 8.0, OP.is_lt, 16.0, OP.mult); ts(col(7), v("E16", 0, 1), float(ZC), OP.mult)
    act(v("S32"), v("SEL"), scale=32.0); act(v("SM"), v("SEL"), scale=-1.0); iota(v("N2"), [[2, 256]], 2, 0)
    for n, c in (("SN", 4), ("SW", 5), ("SP", 9)): act(v(n), v("SEL"), scale=col(c))
    for k in range(4): ms(v("W", 1056 * k, 1056 * k + 1056), 0.0)
    act(v("PADC"), v("ZERO"), AF.Identity, bias=col(7)); act(v("W", ZC), v("PADC"))
    ms(v("OK", 0, 128), 1.0)
    for k in range(2): act(v("ZV", 256 * k, 256 * k + 256), v("ZERO"), AF.Silu, bias=col(14))
    ts(v("NLI"), v("NLI"), col(2), OP.add); ts(v("DUM"), v("DUM"), col(2), OP.add)
    ts(v("K1"), v("NLI"), -float(O), OP.add); ts(v("K2"), v("NLI"), float(ZC), OP.add, 1.0 / 128, OP.mult)
    ms(v("CUM"), 1024.0); ms(v("CUM", 0, 288, 144), 0.0); ms(v("TW"), 0.0); ms(v("FG"), 0.0)
    for t in range(RO):
        ms(v("X%d" % t, 0, O), 0.0); ms(v("X%d" % t, O + ZC, XW), 0.0)
    ms(v("D", 0, O), 0.0)
    cp(v("HO"), v("HD")); ts(v("HF"), v("HD"), float(EARLY), OP.is_lt, -8192.0, OP.mult); tt(v("HF"), v("HD"), v("HF"), OP.subtract)
    ts(v("HA"), v("HF"), O - 8192.0, OP.add)
    cp(v("GA"), ind(v("X0", 0, O + EARLY), v("HA"))); send("A", v("LA"))
    tt(v("G0"), ind(v("X0", O, O + V), v("HO")), v("GA"), OP.subtract); send("0", v("LB"), [mark("outA")])
    tt(v("X0", O + V, O + ZC), v("LA"), v("LB"), OP.add)
    for b in range(2):
        for h in range(2):
            asel(v("PINV", 128 * (2 * b + h), 128 * (2 * b + h + 1)), [[16, 8], [1, 8], [1000, 2]], 8 * h - 1000 * b, [mark("out0")])
    cp(v("NF"), v("NX"))
    for b in range(2):
        mm(v("P3", 128 * b, 128 * b + 128), [(v("PERM", 128 * (2 * b + h), 128 * (2 * b + h + 1)), v("NF", h, 256, 2)) for h in range(2)])
    ts(v("YL"), v("P3", 0, 256), 0.0, OP.is_lt, ZC + 1.0, OP.mult); tt(v("N"), v("P3", 0, 256), v("YL"), OP.add)
    ts(v("LIVE", 0, 128), v("N", 0, 128), float(ZC), OP.is_lt)
    for k in range(4): spread(0, k)
    cp(v("OFF"), v("N"))
    for k in range(4):
        act(nodes("S0", 1, 512 * k, 512), nodes("X0", 1, 512 * k, 512))
        tt(nodes("S0", 0, 512 * k, 512), nodes("X0", 0, 512 * k, 512), v("P%d" % (4 + k)), OP.mult)

    def scan(i):
        o = 144 * i
        add("V", "c", lambda e: e.tensor_tensor_scan(T.CUM[:, o + 1:o + 129], T.FG[:, o:o + 128], T.FG[:, 288 + o:416 + o], 0.0, OP.add, OP.add),
            v("CUM", o + 1, o + 129), [v("FG", o, o + 128), v("FG", 288 + o, 416 + o)])
    def search():
        mm(v("P1", 2, 4), [(sel(r), v("CUM", 16 * r + 16, 288, 144)) for r in range(8)])
        mm(v("P1", 1, 2), [(v("ONE"), v("CUM", 128, 129))])
        mm(v("P2", 288, 306), rows("CUM", 1, 288))
        mm(v("P4", 0, 288), [(v("LLE"), v("CUM", 1, 289)), (v("LGT"), v("CUM", 0, 288)), (v("IDM"), v("FG", 288, 576))])
        act(v("TW", 0, 288, 16), v("P2", 288, 306)); act(v("RY"), v("P4", 0, 288))
        for i in range(2): ts(v("FL1", 256 * i, 256 * i + 256), v("NROW"), v("P1", 2 + i, 3 + i), OP.is_ge, col(6), OP.mult)
        ts(v("Q"), v("NLI"), v("P1", 1, 2), OP.is_lt, 65536.0, OP.mult)
        c = v("P1", 32, 64)
        mm(c, rows("FL1", 0, 512))
        tt(v("LV"), v("Q"), v("K1"), OP.add); tt(v("LS"), v("K2"), v("Q"), OP.subtract)
        cp(v("OD"), c)
        for i in range(2):
            tt(v("FL2", 256 * i, 256 * i + 256), ind(v("TW", 144 * i, 144 * i + 144), v("OD", 16 * i, 16 * i + 16)), v("NROW"), OP.is_le)
        c = v("P1", 64, 96); mm(c, rows("FL1", 0, 512) + rows("FL2", 0, 512))
        cp(v("OC"), c); ts(v("BV"), c, 32.0, OP.mult); ts(v("BS"), c, 1.0 / 128, OP.mult)
        for i in range(2):
            tt(v("FL3", 256 * i, 256 * i + 256), ind(v("RY", 144 * i, 144 * i + 144), v("OC", 16 * i, 16 * i + 16)), v("N2"), OP.subtract)
        ts(v("FL3", 512, 1024), v("FL3", 0, 512), 0.0, OP.min, -2.0, OP.max)
        mm(v("P1", 96, 128), rows("FL3", 512, 512, "SM"))
        tt(v("BV", 0, 16), v("BV", 0, 16), v("LV"), OP.min); tt(v("BS", 0, 16), v("BS", 0, 16), v("LS"), OP.max)
        tt(v("VV"), v("P1", 96, 128), v("BV"), OP.add); tt(v("SS"), v("P1", 96, 128), v("BS"), OP.add)
        ts(v("OV"), v("VV"), float(O), OP.add); ts(v("OS"), v("SS"), 128.0, OP.mult)
        mm(v("P2", 0, 256), [(sel(0, "S32"), v("FL1", 256, 512)), (sel(0, "S32"), v("FL2", 256, 512)), (sel(1, "SM"), v("FL3", 768, 1024))])
    def freed():
        ts(v("T3"), v("ZL", 128, 256), 1.0, OP.is_gt, float(ZC), OP.mult); tt(v("N", 128, 256), v("P0", 384, 512), v("T3"), OP.max)
    def place(lo, n): return [(v("I128"), v("NL", lo, lo + n)), (v("I32"), v("NH", lo, lo + n))]
    def to_w():
        dma("Y", v("W", 0, V, 1, 0), v("NH"), 1 << 16); dma("Y", v("W", 0, V, 1, 1), v("NL"), 1 << 16)

    ne = v("N", 0, 128)
    for t in range(RO):
        X, Xn, XS, Z = "X%d" % t, "X%d" % (t + 1), "S%d" % t, "Z%d" % t
        win = v(X, O, XW); last = t == RO - 1
        def lengths(b, sizes):
            for lo, n in pieces(sizes):
                tt(nodes("D", b, lo, n), ind(win, v("OFF", 128 * b + lo // 16, 128 * b + (lo + n) // 16)), nodes(XS, b, lo, n), OP.subtract)
                act(v("A", 2048 * b + lo, 2048 * b + lo + n), nodes("D", b, lo, n), AF.Abs)
                mm(v("P0" if b else "P3", 128 + lo // 16, 128 + (lo + n) // 16), rows("A", 2048 * b + lo, n))
        def move(b, k):
            pb = v("P%d" % (5 + (k + b) % 3))
            mm(pb, [(v("ID"), nodes(XS, b, 512 * k, 512)), (v("ID"), v("C", 2048 * b + 512 * k, 2048 * b + 512 * k + 512))])
            act(nodes(Xn, b, 512 * k, 512), pb)
        ts(v("T1"), ne, -15.5, OP.add, M32, OP.add); act(v("NH", 0, 128), v("T1"), AF.Identity, bias=col(15)); act(v("NH", 128, 256), v("N", 128, 256))
        act(v("NOTO"), ne, AF.Relu, bias=col(8))
        mm(v("P2", 0, 256), [(v("IDF"), v("N")), (v("IDM"), v("NH"))]); act(v("NL"), v("P2", 0, 256)); to_w()
        mm(v("P4", 384, 512), place(0, 128)); cp(v("SIG"), v("P4", 384, 512))
        dma("Y", v(Z, 2048, None, 1, 0), v("ZERO"), 1 << 17, [v("NL")])
        lengths(1, ODD)
        act(v("OK", 128, 256), v("P0", 128, 256), AF.Relu, bias=col(11))
        dma("Y", v("W", 0, V, 1, 2), v("OK"), 1 << 16)
        for k in range(2):
            if k < SIGN: act(v("C", 2048 + 1024 * k, 3072 + 1024 * k), nodes("D", 1, 1024 * k, 1024), AF.Sign)
            else: ts(v("C", 2048 + 1024 * k, 3072 + 1024 * k), nodes("D", 1, 1024 * k, 1024), 1.0, OP.min, -1.0, OP.max)
        if t: freed()
        act(v("FG", 144, 272), ne, AF.Relu, bias=v("HG", 0, 1)); act(v("FG", 432, 560), v("N", 128, 256), AF.Relu, bias=v("HG", 0, 1))
        act(v("THO"), v("FG", 432, 560), AF.Identity, bias=v("HG", 1, 2), scale=8192.0)
        tt(v("FG", 288, 416), v("P0", 128, 256), v("THO"), OP.is_gt); scan(1)
        lengths(0, EVEN)
        ts(v("FG", 0, 128), v("P3", 128, 256), 480.0, OP.is_gt); act(v("NOTS"), v("P3", 128, 256), AF.Relu, bias=col(10)); scan(0)
        for k in range(2): act(v("WG", 1024 * k, 1024 * k + 1024), ind(v("W"), v("SIG", 64 * k, 64 * k + 64)))
        for k in range(2):
            a, b = 64 * k, 64 * k + 64; pen = [(v("IDK"), v(n, a, b)) for n in ("NOTO", "NOTS")]
            mm(v("P3", a, b), pen + [(v("IDM"), v(n, a, b)) for n in ("NH", "NL")] + rows("WG", 1024 * k, 1024, "SW"))
            mm(v("P0", a, b), pen + place(a, 64) + rows("WG", 1024 * k, 1024, "SP"))
        pm = v("P3", 0, 128)
        ts(v("M8"), pm, -8192.0, OP.is_gt); tt(v("DL"), pm, v("M8"), OP.mult); tt(v("NM"), ne, v("DL"), OP.add); cp(v("OF2"), v("NM"))
        tt(v("T2"), v("P0", 0, 128), v("DUM"), OP.max); ts(v("ZO"), v("T2"), 2048.0, OP.add)
        for k in range(4): act(ind(v(Z), v("ZO", 32 * k, 32 * k + 32)), v("ZV"), AF.Silu)
        dma("Y", v("ZL"), v(Z, 2048, None, 1, 0), 1 << 17)
        for k in range(4): move(1, k)
        search()
        for lo, n in pieces(EVEN):
            tt(v("D2", lo, lo + n), ind(win, v("OF2", lo // 16, (lo + n) // 16)), nodes(XS, 0, lo, n), OP.subtract)
            ts(v("C", lo, lo + n), v("D2", lo, lo + n), 1.0, OP.min, -1.0, OP.max)
            for k in range(lo // 512, (lo + n) // 512): move(0, k)
        oi = v("OV", 0, 16); xi = ind(v(X, 0, O + V), oi); di = ind(v("D"), oi); wi = ind(v("W"), v("OS", 0, 16))
        act(v("E1", 0, 256), xi); act(v("VAL", 0, 256), v("P2", 0, 256)); act(v("VAL", 256, 512), wi)
        ts(v("H", 0, 256), di, -0.5, OP.add, MAG, OP.add); ts(v("H", 256, 512), di, 0.5, OP.add, MAG, OP.add)
        act(v("HU"), v("H", 0, 256), AF.Identity, bias=col(13), scale=0.5); act(v("E2"), v("H"), AF.Sign, bias=col(12))
        tt(v("E1", 256, 512), xi, v("HU"), OP.add)
        if t:
            act(v("NH", 128, 256), v("N", 128, 256)); tt(v("NL", 128, 256), v("N", 128, 256), v("NH", 128, 256), OP.subtract); to_w()
        tt(ind(v(Xn, 0, O + V), v("OV")), v("E1"), v("E2"), OP.add)
        if not last:
            G = "G%d" % (t + 1)
            cp(v(G), ind(v(Xn, O, O + V), v("HO"))); send(str(t + 1), v(Xn, O + V, O + ZC))
            for k in range(4): dma("Y", v("S%d" % (t + 1), 1024 * k, 1024 * k + 1024), v(Xn, O + 1024 * k, O + 1024 * k + 1024), 1 << 18, [v(G)])
        cp(ind(v("W"), v("OS")), v("VAL"))
        for b, pb in ((1, v("P0", 384, 512)), (0, v("P3", 256, 384))):
            mm(pb, [(sel(r, "SN"), v("W", 256 * r + 128 * b, 256 * r + 128 * b + 128)) for r in range(16)])
        if not last:
            cp(v("OFF", 128, 256), v("P0", 384, 512)); act(v("N", 128, 256), v("P0", 384, 512)); act(v("W", ZC), v("PADC"))
        tt(ne, v("P3", 256, 384), v("DL"), OP.add)
        if not last: cp(v("OFF", 0, 128), ne)

    freed(); ts(v("LIVE", 128, 256), v("N", 128, 256), float(ZC), OP.is_lt)
    ts(v("YL"), v("N"), float(ZC), OP.is_ge, -(ZC + 1.0), OP.mult); tt(v("YL"), v("YL"), v("N"), OP.add)
    for h in range(2):
        mm(v("P1", 128 * h, 128 * h + 128), [(v("PINV", 128 * (2 * b + h), 128 * (2 * b + h + 1)), v("YL", 128 * b, 128 * b + 128)) for b in range(2)])
    for h in range(2): act(v("YO", h, 256, 2), v("P1", 128 * h, 128 * h + 128))
    dma("S", hbm("yn"), v("YO"), 1 << 17)
    for k in range(4):
        spread(1, k)
        tt(nodes("X3", 1, 512 * k, 512), nodes("X3", 1, 512 * k, 512), v("P%d" % (4 + k)), OP.mult)
        dma("Y", hbm("yx", 1024 * k, 1024 * k + 1024), v("X3", O + 1024 * k, O + 1024 * k + 1024), 1 << 18)
    emit(g, T, arrange(ops, ORDER))
    g.wait_ge(T.sem.sent, (RO + 1) * n_out)
